import numpy as np
import ml_dtypes


def mxq(x, axis, fmt="e4m3"):
    dtype, down = {"e4m3": (ml_dtypes.float8_e4m3fn, 7), "e5m2": (ml_dtypes.float8_e5m2, 14)}[fmt]
    v = np.moveaxis(np.asarray(x, np.float32).astype(ml_dtypes.bfloat16).astype(np.float64), axis, -1)
    blocks = v.reshape(v.shape[:-1] + (-1, 32))
    amax = np.abs(blocks).max(-1, keepdims=True)
    byte = np.maximum(np.where(amax > 0, np.frexp(amax)[1] - 1 + 127, 0) - down, 1)
    scale = np.exp2(byte - 127.0)
    codes = (blocks / scale).astype(np.float32).astype(dtype).astype(np.float64)
    return np.moveaxis((codes * scale).reshape(v.shape), -1, axis)


WIDE = False


def mx_kscale(k):
    if not WIDE:
        return np.ones(k)
    levels = np.array([30, -30])
    if k % 512:
        return np.exp2(np.random.permutation(np.resize(levels, k // 32))).repeat(32)
    a = np.empty((k // 512, 16))
    for p in range(k // 512):
        a[p, :8] = np.random.permutation(np.resize(levels, 8))
        for g in range(8):
            far = levels[np.abs(levels - a[p, g]) >= 10]
            a[p, g + 8] = far[np.random.randint(len(far))]
    return np.exp2(a.ravel()).repeat(32)


def f64(x):
    return np.asarray(x).astype(np.float64)


def striped(idx):
    return np.tile(np.asarray(idx).reshape(-1, 16).T, (8, 1)).astype(np.uint16)


def unstriped(offs):
    return offs[:16].T.reshape(-1).astype(np.int64)


E2M1 = np.array([0.0, 0.5, 1.0, 1.5, 2.0, 3.0, 4.0, 6.0, -0.0, -0.5, -1.0, -1.5, -2.0, -3.0, -4.0, -6.0])


def pack_weight(w, fmt):
    k, n = w.shape
    w = f64(np.asarray(w, np.float32).astype(ml_dtypes.bfloat16)).reshape(k // 32, 32, n)
    amax = np.abs(w).max(1)
    if fmt in ("e4m3", "e5m2"):
        byte = np.frexp(amax)[1] - 1 + 127 - (7 if fmt == "e4m3" else 14)
    else:
        mant, ex = np.frexp(amax / 6.0)
        byte = np.where(mant > 0.5, ex, ex - 1) + 127
    byte = np.clip(np.where(amax > 0, byte, 1), 1, 254)
    scaled = (w * np.exp2(127.0 - byte)[:, None, :]).reshape(k, n).astype(np.float32)
    by_word = np.ascontiguousarray(scaled.reshape(k // 512, 128, 4, n).transpose(0, 1, 3, 2))
    if fmt in ("e4m3", "e5m2"):
        words = by_word.astype(ml_dtypes.float8_e4m3fn if fmt == "e4m3" else ml_dtypes.float8_e5m2).view(np.uint8)
    else:
        c = by_word.astype(ml_dtypes.float4_e2m1fn).view(np.uint8) & 0xF
        words = (c[..., 0::2] | (c[..., 1::2] << 4)).reshape(k // 512, 128, 2 * n)
    return np.ascontiguousarray(words), np.ascontiguousarray(byte.astype(np.uint8).reshape(k // 512, 16, n))


def unpack_weight(words, scales, fmt):
    g, _, n = scales.shape
    words = np.ascontiguousarray(words).reshape(g, 128, n, -1)
    if fmt in ("e4m3", "e5m2"):
        vals = words.view(ml_dtypes.float8_e4m3fn if fmt == "e4m3" else ml_dtypes.float8_e5m2).astype(np.float64)
    else:
        nib = np.empty((g, 128, n, 4), np.uint8)
        nib[..., 0::2] = words & 0xF
        nib[..., 1::2] = words >> 4
        vals = E2M1[nib]
    vals = vals * np.repeat(np.exp2(scales.astype(np.float64) - 127.0), 8, axis=1)[..., None]
    return vals.transpose(0, 1, 3, 2).reshape(g * 512, n)


def bf(x):
    return np.asarray(x, np.float32).astype(ml_dtypes.bfloat16)


def planes(Y):
    r, m = Y.shape
    b = f64(bf(Y)).reshape(r // 32, 32, m)
    amax = np.abs(b).max(1)
    byte = np.clip(np.where(amax > 0, np.frexp(amax)[1] - 1 + 127 - 7, 1), 1, 254)
    codes = (b * np.exp2(127.0 - byte)[:, None, :]).reshape(r, m).astype(np.float32).astype(ml_dtypes.float8_e4m3fn).view(np.uint8)
    words = codes.reshape(r // 512, 128, 4, m).transpose(0, 1, 3, 2)
    return np.ascontiguousarray(words), np.ascontiguousarray(byte.astype(np.uint8).reshape(r // 512, 16, m))


K, T, J, R, N, C = 1024, 1024, 384, 512, 512, 1024


def setup_inputs():
    n = np.random.standard_normal
    idx = np.random.permutation(T)[:J]
    idx2 = np.random.permutation(T)[:J]
    idx3 = np.random.permutation(C)[:J]
    fk = mx_kscale(K)
    fr = mx_kscale(R)
    wp = pack_weight(n((K, R)) * 1 / np.sqrt(K) * fk[:, None] * fr, "e5m2")
    wbp = pack_weight(n((R, N)) * 1 / np.sqrt(R) / fr[:, None], "e2m1")
    return {
        "xf": (n((K, T))).astype(np.float32),
        "fk": (np.random.uniform(0.5, 2.0, (K, 1)) / fk[:, None]).astype(np.float32),
        "w_words": wp[0],
        "w_scales": wp[1],
        "us": (np.random.uniform(0.5, 2.0, (R, 1)) * fr[:, None]).astype(np.float32),
        "wb_words": wbp[0],
        "wb_scales": wbp[1],
        "old": (1.0 * n((N, C))).astype(np.float32),
        "offs": striped(idx),
        "offs2": striped(idx2),
        "offs3": striped(idx3),
    }


def reference(xf, fk, w_words, w_scales, us, wb_words, wb_scales, old, offs, offs2, offs3):
    idx = unstriped(offs)
    idx2 = unstriped(offs2)
    idx3 = unstriped(offs3)
    wu = unpack_weight(w_words, w_scales, "e5m2")
    wbu = unpack_weight(wb_words, wb_scales, "e2m1")
    u = (f64(xf)[:, idx] - f64(xf)[:, idx2]) * f64(fk)
    uq = mxq(u, 0, "e4m3")
    a = wu.T @ uq
    pk1 = np.max(np.abs(a), axis=1, keepdims=True)
    hid = a / pk1 * f64(us)
    hidq = mxq(hid, 0, "e4m3")
    p = wbu.T @ hidq
    pp = np.zeros((N, C))
    pp[:, idx3] = p
    y = pp + 0.5 * f64(old)
    words, scales = planes(y)
    return y, words, scales

@@ -1,0 +1,265 @@
+from contextlib import ExitStack
+
+import concourse.mybir as mybir
+
+K, T, J, R, N, C = 1024, 1024, 384, 512, 512, 1024
+FLOPS = 2 * K * R * J + 2 * R * N * J
+
+F32 = mybir.dt.float32
+BF16 = mybir.dt.bfloat16
+I32 = mybir.dt.int32
+U32 = mybir.dt.uint32
+U16 = mybir.dt.uint16
+U8 = mybir.dt.uint8
+E4M3 = mybir.dt.float8_e4m3fn_x4
+E5M2 = mybir.dt.float8_e5m2_x4
+E2M1 = mybir.dt.float4_e2m1fn_x4
+ALU = mybir.AluOpType
+ACT = mybir.ActivationFunctionType
+AX = mybir.AxisListType
+
+P = 128
+PACK = 4
+PASSES = K // (P * PACK)
+CH = 128
+CHUNKS = J // CH
+OC = CH // 16
+
+
+def tile_list_pickgaps_peakscaled_scattered_pl_kernel(
+    tc, xf, fk, w_words, w_scales, us, wb_words, wb_scales, old, offs, offs2, offs3, out_0, out_1, out_2
+):
+    nc = tc.nc
+    with ExitStack() as ctx:
+        keep = ctx.enter_context(tc.tile_pool(name="keep", bufs=1))
+        psum = ctx.enter_context(tc.psum_pool(name="psum", bufs=1))
+
+        first = keep.tile([P, J // 16], U16, name="first")
+        second = keep.tile([P, J // 16], U16, name="second")
+        places = keep.tile([P, J // 16], U16, name="places")
+        x = [keep.tile([P, T], F32, name=f"x{i}") for i in range(PASSES * PACK)]
+        w_raw = [keep.tile([P, R], U32, name=f"w_raw{a}") for a in range(PASSES)]
+        wb_raw = keep.tile([P, N], U16, name="wb_raw")
+        olds = [keep.tile([P, C], F32, name=f"old{t}") for t in range(PACK)]
+        fk_sb = keep.tile([P, PASSES, PACK], F32, name="fk_sb")
+        us_sb = keep.tile([P, PACK], F32, name="us_sb")
+        ws_raw = keep.tile([P, PASSES, R], U8, name="ws_raw")
+        wbs_raw = keep.tile([P, N], U8, name="wbs_raw")
+
+        xf_rows = xf.rearrange("(a p t) c -> a t p c", a=PASSES, t=PACK)
+        old_rows = old.rearrange("(p t) c -> t p c", t=PACK)
+        out_rows = out_0.rearrange("(p t) c -> t p c", t=PACK)
+
+        def load_w(a):
+            nc.sync.dma_start(w_raw[a][:].bitcast(I32), w_words[a].rearrange("p n t -> p (n t)").bitcast(I32))
+
+        nc.vector.memset(ws_raw[:].bitcast(I32), 0)
+        nc.vector.memset(wbs_raw[:].bitcast(I32), 0)
+        pages = [keep.tile([P, C], F32, name=f"page{t}") for t in range(PACK)]
+        nc.gpsimd.dma_start(fk_sb[:], fk.rearrange("(a p t) o -> p a (t o)", a=PASSES, t=PACK))
+        for t in range(PACK):
+            nc.gpsimd.memset(pages[t][:], 0.0)
+        nc.gpsimd.dma_start(us_sb[:], us.rearrange("(p t) o -> p (t o)", t=PACK))
+
+        nc.sync.dma_start(second[:], offs2)
+        nc.sync.dma_start(x[0][:], xf_rows[0, 0])
+        for q in range(4):
+            nc.sync.dma_start(
+                ws_raw[32 * q : 32 * q + 4].bitcast(I32),
+                w_scales[:, 4 * q : 4 * q + 4, :].rearrange("a r n -> r a n").bitcast(I32),
+            )
+        nc.sync.dma_start(first[:], offs)
+        for t in range(1, PACK):
+            nc.sync.dma_start(x[t][:], xf_rows[0, t])
+        load_w(0)
+        for t in range(PACK):
+            nc.sync.dma_start(x[PACK + t][:], xf_rows[1, t])
+        load_w(1)
+        nc.sync.dma_start(wb_raw[:].bitcast(I32), wb_words[0].bitcast(I32))
+        for q in range(4):
+            nc.sync.dma_start(
+                wbs_raw[32 * q : 32 * q + 4].bitcast(I32), wb_scales[0, 4 * q : 4 * q + 4, :].bitcast(I32)
+            )
+        nc.sync.dma_start(places[:], offs3)
+        for t in range(PACK):
+            nc.sync.dma_start(olds[t][:], old_rows[t])
+
+        w_codes = [keep.tile([P, PACK, P], U32, name=f"w_codes{a}", align_bytes=64) for a in range(PASSES)]
+        w_plane = keep.tile([P, PASSES, PACK, P], U8, name="w_plane", align_bytes=64)
+        wb_codes = keep.tile([P, PACK, P], U16, name="wb_codes", align_bytes=64)
+        wb_plane = keep.tile([P, PACK, P], U8, name="wb_plane", align_bytes=64)
+
+        def deal_w(a):
+            nc.scalar.copy(w_codes[a][:], w_raw[a][:].rearrange("p (m t) -> p t m", t=PACK))
+
+        taken = [keep.tile([P, J], F32, name=f"taken{i}") for i in range(PASSES * PACK)]
+        gaps = [keep.tile([P, PACK, J], F32, name=f"gaps{a}") for a in range(PASSES)]
+        u_bf = [keep.tile([P, J, PACK], BF16, name=f"u_bf{a}", align_bytes=64) for a in range(PASSES)]
+        u_codes = [keep.tile([P, J], U32, name=f"u_codes{a}", align_bytes=64) for a in range(PASSES)]
+        u_plane = [keep.tile([P, J], U8, name=f"u_plane{a}", align_bytes=64) for a in range(PASSES)]
+        a_banks = [psum.tile([P, PACK, CH], F32, name=f"a_bank{c}") for c in range(CHUNKS)]
+        p_banks = [psum.tile([P, PACK, CH], F32, name=f"p_bank{c}") for c in range(CHUNKS)]
+
+        def gather(a, t, lo, hi):
+            i = PACK * a + t
+            nc.scalar.activation(taken[i][:, lo:hi], x[i][:].indirect(second[:, lo // 16 : hi // 16]), ACT.Copy)
+            nc.vector.tensor_tensor(
+                gaps[a][:, t, lo:hi], x[i][:].indirect(first[:, lo // 16 : hi // 16]), taken[i][:, lo:hi], ALU.subtract
+            )
+
+        def weave_u(a, lo, hi):
+            nc.vector.tensor_tensor(
+                u_bf[a][:, lo:hi, :].rearrange("p (c i) t -> p c t i", i=4),
+                gaps[a][:, :, lo:hi].rearrange("p t (c i) -> p c t i", i=4),
+                fk_sb[:, a, :].unsqueeze(1).unsqueeze(3).to_broadcast([P, (hi - lo) // 4, PACK, 4]),
+                ALU.mult,
+            )
+
+        def quantize_u(a, lo, hi):
+            nc.vector.quantize_mx(
+                out=u_codes[a][:, lo:hi].bitcast(E4M3),
+                scales=u_plane[a][:, lo:hi],
+                in_=u_bf[a][:, lo:hi, :].rearrange("p j t -> p (j t)"),
+            )
+
+        def first_product(a, c):
+            cols = slice(c * CH, (c + 1) * CH)
+            for t in range(PACK):
+                nc.tensor.matmul_mx(
+                    out=a_banks[c][:, t, :],
+                    lhsT=w_codes[a][:, t, :].bitcast(E5M2),
+                    lhsT_scale=w_plane[:, a, t, :],
+                    rhs=u_codes[a][:, cols].bitcast(E4M3),
+                    rhs_scale=u_plane[a][:, cols],
+                    start=(a == 0 and t == 0),
+                    stop=(a == PASSES - 1 and t == PACK - 1),
+                )
+
+        nc.vector.tensor_copy(w_plane[:], ws_raw[:].rearrange("p a (m t) -> p a t m", t=PACK))
+        for t in range(PACK):
+            gather(0, t, 0, J)
+        weave_u(0, 0, J)
+        quantize_u(0, 0, J)
+        deal_w(0)
+        for c in range(CHUNKS):
+            first_product(0, c)
+        for t in range(PACK - 1):
+            gather(1, t, 0, J)
+        sizes = [keep.tile([P, PACK, CH], F32, name=f"sizes{c}") for c in range(CHUNKS)]
+        peaks = keep.tile([P, CHUNKS, PACK], F32, name="peaks")
+        for c in range(CHUNKS):
+            gather(1, PACK - 1, c * CH, (c + 1) * CH)
+        deal_w(1)
+        for c in range(CHUNKS):
+            weave_u(1, c * CH, (c + 1) * CH)
+            if c > 0:
+                quantize_u(1, (c - 1) * CH, c * CH)
+                first_product(1, c - 1)
+        quantize_u(1, J - CH, J)
+        first_product(1, CHUNKS - 1)
+        nc.vector.tensor_copy(wb_plane[:], wbs_raw[:].rearrange("p (m t) -> p t m", t=PACK))
+        for c in range(CHUNKS):
+            nc.scalar.activation(sizes[c][:], a_banks[c][:], ACT.Abs)
+            nc.vector.tensor_reduce(peaks[:, c, :], sizes[c][:], AX.X, ALU.max)
+        nc.scalar.copy(wb_codes[:], wb_raw[:].rearrange("p (m t) -> p t m", t=PACK))
+
+        peak = keep.tile([P, PACK], F32, name="peak")
+        inverse = keep.tile([P, PACK], F32, name="inverse")
+        factor = keep.tile([P, PACK], F32, name="factor")
+        nc.vector.tensor_reduce(peak[:], peaks[:].rearrange("p c t -> p t c"), AX.X, ALU.max)
+        nc.vector.reciprocal(inverse[:], peak[:])
+        nc.vector.tensor_tensor(factor[:], inverse[:], us_sb[:], ALU.mult)
+
+        h_bf = [keep.tile([P, CH, PACK], BF16, name=f"h_bf{c}", align_bytes=64) for c in range(CHUNKS)]
+        h_codes = [keep.tile([P, CH], U32, name=f"h_codes{c}", align_bytes=64) for c in range(CHUNKS)]
+        h_plane = [keep.tile([P, CH], U8, name=f"h_plane{c}", align_bytes=64) for c in range(CHUNKS)]
+        p_sb = [keep.tile([P, PACK, CH], F32, name=f"p_sb{c}") for c in range(CHUNKS)]
+
+        def weave_h(c):
+            nc.vector.tensor_tensor(
+                h_bf[c][:],
+                a_banks[c][:].rearrange("p t j -> p j t"),
+                factor[:].unsqueeze(1).to_broadcast([P, CH, PACK]),
+                ALU.mult,
+            )
+
+        def second_product(c):
+            nc.vector.quantize_mx(
+                out=h_codes[c][:].bitcast(E4M3), scales=h_plane[c][:], in_=h_bf[c][:].rearrange("p j t -> p (j t)")
+            )
+            for t in range(PACK):
+                nc.tensor.matmul_mx(
+                    out=p_banks[c][:, t, :],
+                    lhsT=wb_codes[:, t, :].bitcast(E2M1),
+                    lhsT_scale=wb_plane[:, t, :],
+                    rhs=h_codes[c][:].bitcast(E4M3),
+                    rhs_scale=h_plane[c][:],
+                    start=True,
+                    stop=True,
+                )
+            nc.scalar.copy(p_sb[c][:], p_banks[c][:])
+
+        def scatter(t, c, on_vector):
+            window = pages[t][:].indirect(places[:, c * OC : (c + 1) * OC])
+            if on_vector:
+                nc.vector.tensor_copy(window, p_sb[c][:, t, :])
+            else:
+                nc.scalar.activation(window, p_sb[c][:, t, :], ACT.Copy)
+
+        y = [keep.tile([P, 2, C], F32, name=f"y{u}") for u in range(2)]
+        y_bf = keep.tile([P, C, PACK], BF16, name="y_bf", align_bytes=64)
+        y_codes = keep.tile([P, C], U32, name="y_codes", align_bytes=64)
+        y_plane = keep.tile([P, C], U8, name="y_plane", align_bytes=64)
+
+        def add_old(t, lo, hi):
+            nc.vector.scalar_tensor_tensor(
+                y[t // 2][:, t % 2, lo:hi], olds[t][:, lo:hi], 0.5, pages[t][:, lo:hi], ALU.mult, ALU.add
+            )
+            nc.sync.dma_start(out_rows[t][:, lo:hi], y[t // 2][:, t % 2, lo:hi])
+
+        def round_pair(u, lo, hi, on_vector):
+            dst = y_bf[:, lo:hi, 2 * u : 2 * u + 2]
+            src = y[u][:, :, lo:hi].rearrange("p e c -> p c e")
+            if on_vector:
+                nc.vector.tensor_copy(dst, src)
+            else:
+                nc.scalar.copy(dst, src)
+
+        def quantize_y(lo, hi):
+            nc.vector.quantize_mx(
+                out=y_codes[:, lo:hi].bitcast(E4M3),
+                scales=y_plane[:, lo:hi],
+                in_=y_bf[:, lo:hi, :].rearrange("p c t -> p (c t)"),
+            )
+            nc.sync.dma_start(
+                out_1[0].rearrange("p c t -> p (c t)").bitcast(I32)[:, lo:hi], y_codes[:, lo:hi].bitcast(I32)
+            )
+
+        weave_h(0)
+        for c in range(CHUNKS):
+            if c + 1 < CHUNKS:
+                weave_h(c + 1)
+            second_product(c)
+            scatter(1, c, False)
+        for c in range(CHUNKS):
+            scatter(0, c, True)
+        for c in range(CHUNKS):
+            scatter(2, c, False)
+        add_old(0, 0, C)
+        add_old(1, 0, C)
+        scatter(3, 0, True)
+        scatter(3, 1, True)
+        scatter(3, 2, False)
+        add_old(2, 0, C)
+        half = C // 2
+        round_pair(0, 0, half, False)
+        round_pair(0, half, C, False)
+        add_old(3, 0, half)
+        add_old(3, half, C)
+        round_pair(1, 0, half, True)
+        round_pair(1, half, C, True)
+        quantize_y(0, half)
+        quantize_y(half, C)
+        for q in range(4):
+            queue = nc.sync if q % 2 == 0 else nc.scalar
+            queue.dma_start(out_2[0, 4 * q : 4 * q + 4, :].bitcast(I32), y_plane[32 * q : 32 * q + 4, :].bitcast(I32))

@@ -24,6 +24,9 @@ PASSES = K // (P * PACK)
 CH = 128
 CHUNKS = J // CH
 OC = CH // 16
+BOTH_ON_SCALAR = PACK
+QUARTERS = 4
+QW = C // QUARTERS
 
 
 def tile_list_pickgaps_peakscaled_scattered_pl_kernel(
@@ -48,7 +51,6 @@ def tile_list_pickgaps_peakscaled_scattered_pl_kernel(
 
         xf_rows = xf.rearrange("(a p t) c -> a t p c", a=PASSES, t=PACK)
         old_rows = old.rearrange("(p t) c -> t p c", t=PACK)
-        out_rows = out_0.rearrange("(p t) c -> t p c", t=PACK)
 
         def load_w(a):
             nc.sync.dma_start(w_raw[a][:].bitcast(I32), w_words[a].rearrange("p n t -> p (n t)").bitcast(I32))
@@ -56,10 +58,8 @@ def tile_list_pickgaps_peakscaled_scattered_pl_kernel(
         nc.vector.memset(ws_raw[:].bitcast(I32), 0)
         nc.vector.memset(wbs_raw[:].bitcast(I32), 0)
         pages = [keep.tile([P, C], F32, name=f"page{t}") for t in range(PACK)]
-        nc.gpsimd.dma_start(fk_sb[:], fk.rearrange("(a p t) o -> p a (t o)", a=PASSES, t=PACK))
         for t in range(PACK):
-            nc.gpsimd.memset(pages[t][:], 0.0)
-        nc.gpsimd.dma_start(us_sb[:], us.rearrange("(p t) o -> p (t o)", t=PACK))
+            nc.vector.memset(pages[t][:].bitcast(I32), 0)
 
         nc.sync.dma_start(second[:], offs2)
         nc.sync.dma_start(x[0][:], xf_rows[0, 0])
@@ -69,17 +69,20 @@ def tile_list_pickgaps_peakscaled_scattered_pl_kernel(
                 w_scales[:, 4 * q : 4 * q + 4, :].rearrange("a r n -> r a n").bitcast(I32),
             )
         nc.sync.dma_start(first[:], offs)
-        for t in range(1, PACK):
-            nc.sync.dma_start(x[t][:], xf_rows[0, t])
-        load_w(0)
-        for t in range(PACK):
-            nc.sync.dma_start(x[PACK + t][:], xf_rows[1, t])
-        load_w(1)
-        nc.sync.dma_start(wb_raw[:].bitcast(I32), wb_words[0].bitcast(I32))
+        nc.sync.dma_start(x[1][:], xf_rows[0, 1])
+        nc.sync.dma_start(x[2][:], xf_rows[0, 2])
+        nc.sync.dma_start(x[3][:], xf_rows[0, 3])
         for q in range(4):
             nc.sync.dma_start(
                 wbs_raw[32 * q : 32 * q + 4].bitcast(I32), wb_scales[0, 4 * q : 4 * q + 4, :].bitcast(I32)
             )
+        nc.sync.dma_start(fk_sb[:], fk.rearrange("(a p t) o -> p a (t o)", a=PASSES, t=PACK))
+        for t in range(PACK):
+            nc.sync.dma_start(x[PACK + t][:], xf_rows[1, t])
+        load_w(0)
+        load_w(1)
+        nc.sync.dma_start(wb_raw[:].bitcast(I32), wb_words[0].bitcast(I32))
+        nc.sync.dma_start(us_sb[:], us.rearrange("(p t) o -> p (t o)", t=PACK))
         nc.sync.dma_start(places[:], offs3)
         for t in range(PACK):
             nc.sync.dma_start(olds[t][:], old_rows[t])
@@ -93,6 +96,7 @@ def tile_list_pickgaps_peakscaled_scattered_pl_kernel(
             nc.scalar.copy(w_codes[a][:], w_raw[a][:].rearrange("p (m t) -> p t m", t=PACK))
 
         taken = [keep.tile([P, J], F32, name=f"taken{i}") for i in range(PASSES * PACK)]
+        kept = keep.tile([P, J], F32, name="kept")
         gaps = [keep.tile([P, PACK, J], F32, name=f"gaps{a}") for a in range(PASSES)]
         u_bf = [keep.tile([P, J, PACK], BF16, name=f"u_bf{a}", align_bytes=64) for a in range(PASSES)]
         u_codes = [keep.tile([P, J], U32, name=f"u_codes{a}", align_bytes=64) for a in range(PASSES)]
@@ -103,23 +107,25 @@ def tile_list_pickgaps_peakscaled_scattered_pl_kernel(
         def gather(a, t, lo, hi):
             i = PACK * a + t
             nc.scalar.activation(taken[i][:, lo:hi], x[i][:].indirect(second[:, lo // 16 : hi // 16]), ACT.Copy)
-            nc.vector.tensor_tensor(
-                gaps[a][:, t, lo:hi], x[i][:].indirect(first[:, lo // 16 : hi // 16]), taken[i][:, lo:hi], ALU.subtract
-            )
+            minuend = x[i][:].indirect(first[:, lo // 16 : hi // 16])
+            if i == BOTH_ON_SCALAR:
+                nc.scalar.activation(kept[:, lo:hi], minuend, ACT.Copy)
+                minuend = kept[:, lo:hi]
+            nc.vector.tensor_tensor(gaps[a][:, t, lo:hi], minuend, taken[i][:, lo:hi], ALU.subtract)
 
-        def weave_u(a, lo, hi):
+        def weave_u(a, lo, hi, rounded):
             nc.vector.tensor_tensor(
-                u_bf[a][:, lo:hi, :].rearrange("p (c i) t -> p c t i", i=4),
+                rounded.rearrange("p (c i) t -> p c t i", i=4),
                 gaps[a][:, :, lo:hi].rearrange("p t (c i) -> p c t i", i=4),
                 fk_sb[:, a, :].unsqueeze(1).unsqueeze(3).to_broadcast([P, (hi - lo) // 4, PACK, 4]),
                 ALU.mult,
             )
 
-        def quantize_u(a, lo, hi):
+        def quantize_u(a, lo, hi, rounded):
             nc.vector.quantize_mx(
                 out=u_codes[a][:, lo:hi].bitcast(E4M3),
                 scales=u_plane[a][:, lo:hi],
-                in_=u_bf[a][:, lo:hi, :].rearrange("p j t -> p (j t)"),
+                in_=rounded.rearrange("p j t -> p (j t)"),
             )
 
         def first_product(a, c):
@@ -138,35 +144,34 @@ def tile_list_pickgaps_peakscaled_scattered_pl_kernel(
         nc.vector.tensor_copy(w_plane[:], ws_raw[:].rearrange("p a (m t) -> p a t m", t=PACK))
         for t in range(PACK):
             gather(0, t, 0, J)
-        weave_u(0, 0, J)
-        quantize_u(0, 0, J)
+        weave_u(0, 0, J, u_bf[0][:])
+        nc.vector.tensor_copy(wb_plane[:], wbs_raw[:].rearrange("p (m t) -> p t m", t=PACK))
+        quantize_u(0, 0, J, u_bf[0][:])
+        for t in range(PACK - 1):
+            gather(1, t, 0, J)
+        sizes = [keep.tile([P, PACK, CH], F32, name=f"sizes{c}") for c in range(CHUNKS - 1)]
+        last_sizes = keep.tile([P, PACK, CH + CHUNKS - 1], F32, name="last_sizes")
+        peak = keep.tile([P, PACK], F32, name="peak")
+        for c in range(CHUNKS):
+            lo, hi = c * CH, (c + 1) * CH
+            gather(1, PACK - 1, lo, hi)
+            weave_u(1, lo, hi, u_bf[1][:, lo:hi, :])
+            quantize_u(1, lo, hi, u_bf[1][:, lo:hi, :])
         deal_w(0)
         for c in range(CHUNKS):
             first_product(0, c)
-        for t in range(PACK - 1):
-            gather(1, t, 0, J)
-        sizes = [keep.tile([P, PACK, CH], F32, name=f"sizes{c}") for c in range(CHUNKS)]
-        peaks = keep.tile([P, CHUNKS, PACK], F32, name="peaks")
-        for c in range(CHUNKS):
-            gather(1, PACK - 1, c * CH, (c + 1) * CH)
         deal_w(1)
         for c in range(CHUNKS):
-            weave_u(1, c * CH, (c + 1) * CH)
-            if c > 0:
-                quantize_u(1, (c - 1) * CH, c * CH)
-                first_product(1, c - 1)
-        quantize_u(1, J - CH, J)
-        first_product(1, CHUNKS - 1)
-        nc.vector.tensor_copy(wb_plane[:], wbs_raw[:].rearrange("p (m t) -> p t m", t=PACK))
-        for c in range(CHUNKS):
-            nc.scalar.activation(sizes[c][:], a_banks[c][:], ACT.Abs)
-            nc.vector.tensor_reduce(peaks[:, c, :], sizes[c][:], AX.X, ALU.max)
+            first_product(1, c)
         nc.scalar.copy(wb_codes[:], wb_raw[:].rearrange("p (m t) -> p t m", t=PACK))
+        for c in range(CHUNKS - 1):
+            nc.scalar.activation(sizes[c][:], a_banks[c][:], ACT.Abs)
+            nc.vector.tensor_reduce(last_sizes[:, :, CH + c], sizes[c][:], AX.X, ALU.max)
+        nc.scalar.activation(last_sizes[:, :, 0:CH], a_banks[CHUNKS - 1][:], ACT.Abs)
+        nc.vector.tensor_reduce(peak[:], last_sizes[:], AX.X, ALU.max)
 
-        peak = keep.tile([P, PACK], F32, name="peak")
         inverse = keep.tile([P, PACK], F32, name="inverse")
         factor = keep.tile([P, PACK], F32, name="factor")
-        nc.vector.tensor_reduce(peak[:], peaks[:].rearrange("p c t -> p t c"), AX.X, ALU.max)
         nc.vector.reciprocal(inverse[:], peak[:])
         nc.vector.tensor_tensor(factor[:], inverse[:], us_sb[:], ALU.mult)
 
@@ -206,60 +211,62 @@ def tile_list_pickgaps_peakscaled_scattered_pl_kernel(
             else:
                 nc.scalar.activation(window, p_sb[c][:, t, :], ACT.Copy)
 
-        y = [keep.tile([P, 2, C], F32, name=f"y{u}") for u in range(2)]
-        y_bf = keep.tile([P, C, PACK], BF16, name="y_bf", align_bytes=64)
+        y = [keep.tile([P, PACK, QW], F32, name=f"y{q}") for q in range(QUARTERS)]
+        y_bf = [keep.tile([P, QW, PACK], BF16, name=f"y_bf{q}", align_bytes=64) for q in range(QUARTERS)]
         y_codes = keep.tile([P, C], U32, name="y_codes", align_bytes=64)
         y_plane = keep.tile([P, C], U8, name="y_plane", align_bytes=64)
+        out_rows = out_0.rearrange("(p t) c -> p t c", t=PACK)
 
-        def add_old(t, lo, hi):
-            nc.vector.scalar_tensor_tensor(
-                y[t // 2][:, t % 2, lo:hi], olds[t][:, lo:hi], 0.5, pages[t][:, lo:hi], ALU.mult, ALU.add
-            )
-            nc.sync.dma_start(out_rows[t][:, lo:hi], y[t // 2][:, t % 2, lo:hi])
+        def add_old(t, q):
+            cols = slice(q * QW, (q + 1) * QW)
+            nc.vector.scalar_tensor_tensor(y[q][:, t, :], olds[t][:, cols], 0.5, pages[t][:, cols], ALU.mult, ALU.add)
 
-        def round_pair(u, lo, hi, on_vector):
-            dst = y_bf[:, lo:hi, 2 * u : 2 * u + 2]
-            src = y[u][:, :, lo:hi].rearrange("p e c -> p c e")
+        def store_pair(u, q):
+            nc.sync.dma_start(out_rows[:, 2 * u : 2 * u + 2, q * QW : (q + 1) * QW], y[q][:, 2 * u : 2 * u + 2, :])
+
+        def round_y(q, on_vector):
+            dst = y_bf[q][:].rearrange("p (c i) t -> p c t i", i=4)
+            src = y[q][:].rearrange("p t (c i) -> p c t i", i=4)
             if on_vector:
                 nc.vector.tensor_copy(dst, src)
             else:
                 nc.scalar.copy(dst, src)
 
-        def quantize_y(lo, hi):
+        def quantize_y(q):
+            cols = slice(q * QW, (q + 1) * QW)
             nc.vector.quantize_mx(
-                out=y_codes[:, lo:hi].bitcast(E4M3),
-                scales=y_plane[:, lo:hi],
-                in_=y_bf[:, lo:hi, :].rearrange("p c t -> p (c t)"),
+                out=y_codes[:, cols].bitcast(E4M3),
+                scales=y_plane[:, cols],
+                in_=y_bf[q][:].rearrange("p c t -> p (c t)"),
             )
-            nc.sync.dma_start(
-                out_1[0].rearrange("p c t -> p (c t)").bitcast(I32)[:, lo:hi], y_codes[:, lo:hi].bitcast(I32)
-            )
+            nc.sync.dma_start(out_1[0].rearrange("p c t -> p (c t)").bitcast(I32)[:, cols], y_codes[:, cols].bitcast(I32))
 
-        weave_h(0)
         for c in range(CHUNKS):
-            if c + 1 < CHUNKS:
-                weave_h(c + 1)
+            weave_h(c)
             second_product(c)
             scatter(1, c, False)
         for c in range(CHUNKS):
             scatter(0, c, True)
+        scatter(3, 2, True)
+        scatter(3, 1, True)
         for c in range(CHUNKS):
             scatter(2, c, False)
-        add_old(0, 0, C)
-        add_old(1, 0, C)
-        scatter(3, 0, True)
-        scatter(3, 1, True)
-        scatter(3, 2, False)
-        add_old(2, 0, C)
-        half = C // 2
-        round_pair(0, 0, half, False)
-        round_pair(0, half, C, False)
-        add_old(3, 0, half)
-        add_old(3, half, C)
-        round_pair(1, 0, half, True)
-        round_pair(1, half, C, True)
-        quantize_y(0, half)
-        quantize_y(half, C)
+        scatter(3, 0, False)
+        for q in range(QUARTERS):
+            add_old(0, q)
+            add_old(1, q)
+            store_pair(0, q)
+        for q in range(QUARTERS):
+            add_old(2, q)
+            add_old(3, q)
+            store_pair(1, q)
+            if q + 1 < QUARTERS:
+                round_y(q, False)
+        quantize_y(0)
+        round_y(QUARTERS - 1, True)
+        quantize_y(1)
+        quantize_y(3)
+        quantize_y(2)
         for q in range(4):
             queue = nc.sync if q % 2 == 0 else nc.scalar
             queue.dma_start(out_2[0, 4 * q : 4 * q + 4, :].bitcast(I32), y_plane[32 * q : 32 * q + 4, :].bitcast(I32))

from contextlib import ExitStack

import concourse.mybir as mybir

K, T, J, R, N, C = 1024, 1024, 384, 512, 512, 1024
FLOPS = 2 * K * R * J + 2 * R * N * J

F32 = mybir.dt.float32
BF16 = mybir.dt.bfloat16
I32 = mybir.dt.int32
U32 = mybir.dt.uint32
U16 = mybir.dt.uint16
U8 = mybir.dt.uint8
E4M3 = mybir.dt.float8_e4m3fn_x4
E5M2 = mybir.dt.float8_e5m2_x4
E2M1 = mybir.dt.float4_e2m1fn_x4
ALU = mybir.AluOpType
ACT = mybir.ActivationFunctionType
AX = mybir.AxisListType

P = 128
PACK = 4
PASSES = K // (P * PACK)
CH = 128
CHUNKS = J // CH
OC = CH // 16
BOTH_ON_SCALAR = PACK
QUARTERS = 4
QW = C // QUARTERS


def tile_list_pickgaps_peakscaled_scattered_pl_kernel(
    tc, xf, fk, w_words, w_scales, us, wb_words, wb_scales, old, offs, offs2, offs3, out_0, out_1, out_2
):
    nc = tc.nc
    with ExitStack() as ctx:
        keep = ctx.enter_context(tc.tile_pool(name="keep", bufs=1))
        psum = ctx.enter_context(tc.psum_pool(name="psum", bufs=1))

        first = keep.tile([P, J // 16], U16, name="first")
        second = keep.tile([P, J // 16], U16, name="second")
        places = keep.tile([P, J // 16], U16, name="places")
        x = [keep.tile([P, T], F32, name=f"x{i}") for i in range(PASSES * PACK)]
        w_raw = [keep.tile([P, R], U32, name=f"w_raw{a}") for a in range(PASSES)]
        wb_raw = keep.tile([P, N], U16, name="wb_raw")
        olds = [keep.tile([P, C], F32, name=f"old{t}") for t in range(PACK)]
        fk_sb = keep.tile([P, PASSES, PACK], F32, name="fk_sb")
        us_sb = keep.tile([P, PACK], F32, name="us_sb")
        ws_raw = keep.tile([P, PASSES, R], U8, name="ws_raw")
        wbs_raw = keep.tile([P, N], U8, name="wbs_raw")

        xf_rows = xf.rearrange("(a p t) c -> a t p c", a=PASSES, t=PACK)
        old_rows = old.rearrange("(p t) c -> t p c", t=PACK)

        def load_w(a):
            nc.sync.dma_start(w_raw[a][:].bitcast(I32), w_words[a].rearrange("p n t -> p (n t)").bitcast(I32))

        nc.vector.memset(ws_raw[:].bitcast(I32), 0)
        nc.vector.memset(wbs_raw[:].bitcast(I32), 0)
        pages = [keep.tile([P, C], F32, name=f"page{t}") for t in range(PACK)]
        for t in range(PACK):
            nc.vector.memset(pages[t][:].bitcast(I32), 0)

        nc.sync.dma_start(second[:], offs2)
        nc.sync.dma_start(x[0][:], xf_rows[0, 0])
        for q in range(4):
            nc.sync.dma_start(
                ws_raw[32 * q : 32 * q + 4].bitcast(I32),
                w_scales[:, 4 * q : 4 * q + 4, :].rearrange("a r n -> r a n").bitcast(I32),
            )
        nc.sync.dma_start(first[:], offs)
        nc.sync.dma_start(x[1][:], xf_rows[0, 1])
        nc.sync.dma_start(x[2][:], xf_rows[0, 2])
        nc.sync.dma_start(x[3][:], xf_rows[0, 3])
        for q in range(4):
            nc.sync.dma_start(
                wbs_raw[32 * q : 32 * q + 4].bitcast(I32), wb_scales[0, 4 * q : 4 * q + 4, :].bitcast(I32)
            )
        nc.sync.dma_start(fk_sb[:], fk.rearrange("(a p t) o -> p a (t o)", a=PASSES, t=PACK))
        for t in range(PACK):
            nc.sync.dma_start(x[PACK + t][:], xf_rows[1, t])
        load_w(0)
        load_w(1)
        nc.sync.dma_start(wb_raw[:].bitcast(I32), wb_words[0].bitcast(I32))
        nc.sync.dma_start(us_sb[:], us.rearrange("(p t) o -> p (t o)", t=PACK))
        nc.sync.dma_start(places[:], offs3)
        for t in range(PACK):
            nc.sync.dma_start(olds[t][:], old_rows[t])

        w_codes = [keep.tile([P, PACK, P], U32, name=f"w_codes{a}", align_bytes=64) for a in range(PASSES)]
        w_plane = keep.tile([P, PASSES, PACK, P], U8, name="w_plane", align_bytes=64)
        wb_codes = keep.tile([P, PACK, P], U16, name="wb_codes", align_bytes=64)
        wb_plane = keep.tile([P, PACK, P], U8, name="wb_plane", align_bytes=64)

        def deal_w(a):
            nc.scalar.copy(w_codes[a][:], w_raw[a][:].rearrange("p (m t) -> p t m", t=PACK))

        taken = [keep.tile([P, J], F32, name=f"taken{i}") for i in range(PASSES * PACK)]
        kept = keep.tile([P, J], F32, name="kept")
        gaps = [keep.tile([P, PACK, J], F32, name=f"gaps{a}") for a in range(PASSES)]
        u_bf = [keep.tile([P, J, PACK], BF16, name=f"u_bf{a}", align_bytes=64) for a in range(PASSES)]
        u_codes = [keep.tile([P, J], U32, name=f"u_codes{a}", align_bytes=64) for a in range(PASSES)]
        u_plane = [keep.tile([P, J], U8, name=f"u_plane{a}", align_bytes=64) for a in range(PASSES)]
        a_banks = [psum.tile([P, PACK, CH], F32, name=f"a_bank{c}") for c in range(CHUNKS)]
        p_banks = [psum.tile([P, PACK, CH], F32, name=f"p_bank{c}") for c in range(CHUNKS)]

        def gather(a, t, lo, hi):
            i = PACK * a + t
            nc.scalar.activation(taken[i][:, lo:hi], x[i][:].indirect(second[:, lo // 16 : hi // 16]), ACT.Copy)
            minuend = x[i][:].indirect(first[:, lo // 16 : hi // 16])
            if i == BOTH_ON_SCALAR:
                nc.scalar.activation(kept[:, lo:hi], minuend, ACT.Copy)
                minuend = kept[:, lo:hi]
            nc.vector.tensor_tensor(gaps[a][:, t, lo:hi], minuend, taken[i][:, lo:hi], ALU.subtract)

        def weave_u(a, lo, hi, rounded):
            nc.vector.tensor_tensor(
                rounded.rearrange("p (c i) t -> p c t i", i=4),
                gaps[a][:, :, lo:hi].rearrange("p t (c i) -> p c t i", i=4),
                fk_sb[:, a, :].unsqueeze(1).unsqueeze(3).to_broadcast([P, (hi - lo) // 4, PACK, 4]),
                ALU.mult,
            )

        def quantize_u(a, lo, hi, rounded):
            nc.vector.quantize_mx(
                out=u_codes[a][:, lo:hi].bitcast(E4M3),
                scales=u_plane[a][:, lo:hi],
                in_=rounded.rearrange("p j t -> p (j t)"),
            )

        def first_product(a, c):
            cols = slice(c * CH, (c + 1) * CH)
            for t in range(PACK):
                nc.tensor.matmul_mx(
                    out=a_banks[c][:, t, :],
                    lhsT=w_codes[a][:, t, :].bitcast(E5M2),
                    lhsT_scale=w_plane[:, a, t, :],
                    rhs=u_codes[a][:, cols].bitcast(E4M3),
                    rhs_scale=u_plane[a][:, cols],
                    start=(a == 0 and t == 0),
                    stop=(a == PASSES - 1 and t == PACK - 1),
                )

        nc.vector.tensor_copy(w_plane[:], ws_raw[:].rearrange("p a (m t) -> p a t m", t=PACK))
        for t in range(PACK):
            gather(0, t, 0, J)
        weave_u(0, 0, J, u_bf[0][:])
        nc.vector.tensor_copy(wb_plane[:], wbs_raw[:].rearrange("p (m t) -> p t m", t=PACK))
        quantize_u(0, 0, J, u_bf[0][:])
        for t in range(PACK - 1):
            gather(1, t, 0, J)
        sizes = [keep.tile([P, PACK, CH], F32, name=f"sizes{c}") for c in range(CHUNKS - 1)]
        last_sizes = keep.tile([P, PACK, CH + CHUNKS - 1], F32, name="last_sizes")
        peak = keep.tile([P, PACK], F32, name="peak")
        for c in range(CHUNKS):
            lo, hi = c * CH, (c + 1) * CH
            gather(1, PACK - 1, lo, hi)
            weave_u(1, lo, hi, u_bf[1][:, lo:hi, :])
            quantize_u(1, lo, hi, u_bf[1][:, lo:hi, :])
        deal_w(0)
        for c in range(CHUNKS):
            first_product(0, c)
        deal_w(1)
        for c in range(CHUNKS):
            first_product(1, c)
        nc.scalar.copy(wb_codes[:], wb_raw[:].rearrange("p (m t) -> p t m", t=PACK))
        for c in range(CHUNKS - 1):
            nc.scalar.activation(sizes[c][:], a_banks[c][:], ACT.Abs)
            nc.vector.tensor_reduce(last_sizes[:, :, CH + c], sizes[c][:], AX.X, ALU.max)
        nc.scalar.activation(last_sizes[:, :, 0:CH], a_banks[CHUNKS - 1][:], ACT.Abs)
        nc.vector.tensor_reduce(peak[:], last_sizes[:], AX.X, ALU.max)

        inverse = keep.tile([P, PACK], F32, name="inverse")
        factor = keep.tile([P, PACK], F32, name="factor")
        nc.vector.reciprocal(inverse[:], peak[:])
        nc.vector.tensor_tensor(factor[:], inverse[:], us_sb[:], ALU.mult)

        h_bf = [keep.tile([P, CH, PACK], BF16, name=f"h_bf{c}", align_bytes=64) for c in range(CHUNKS)]
        h_codes = [keep.tile([P, CH], U32, name=f"h_codes{c}", align_bytes=64) for c in range(CHUNKS)]
        h_plane = [keep.tile([P, CH], U8, name=f"h_plane{c}", align_bytes=64) for c in range(CHUNKS)]
        p_sb = [keep.tile([P, PACK, CH], F32, name=f"p_sb{c}") for c in range(CHUNKS)]

        def weave_h(c):
            nc.vector.tensor_tensor(
                h_bf[c][:],
                a_banks[c][:].rearrange("p t j -> p j t"),
                factor[:].unsqueeze(1).to_broadcast([P, CH, PACK]),
                ALU.mult,
            )

        def second_product(c):
            nc.vector.quantize_mx(
                out=h_codes[c][:].bitcast(E4M3), scales=h_plane[c][:], in_=h_bf[c][:].rearrange("p j t -> p (j t)")
            )
            for t in range(PACK):
                nc.tensor.matmul_mx(
                    out=p_banks[c][:, t, :],
                    lhsT=wb_codes[:, t, :].bitcast(E2M1),
                    lhsT_scale=wb_plane[:, t, :],
                    rhs=h_codes[c][:].bitcast(E4M3),
                    rhs_scale=h_plane[c][:],
                    start=True,
                    stop=True,
                )
            nc.scalar.copy(p_sb[c][:], p_banks[c][:])

        def scatter(t, c, on_vector):
            window = pages[t][:].indirect(places[:, c * OC : (c + 1) * OC])
            if on_vector:
                nc.vector.tensor_copy(window, p_sb[c][:, t, :])
            else:
                nc.scalar.activation(window, p_sb[c][:, t, :], ACT.Copy)

        y = [keep.tile([P, PACK, QW], F32, name=f"y{q}") for q in range(QUARTERS)]
        y_bf = [keep.tile([P, QW, PACK], BF16, name=f"y_bf{q}", align_bytes=64) for q in range(QUARTERS)]
        y_codes = keep.tile([P, C], U32, name="y_codes", align_bytes=64)
        y_plane = keep.tile([P, C], U8, name="y_plane", align_bytes=64)
        out_rows = out_0.rearrange("(p t) c -> p t c", t=PACK)

        def add_old(t, q):
            cols = slice(q * QW, (q + 1) * QW)
            nc.vector.scalar_tensor_tensor(y[q][:, t, :], olds[t][:, cols], 0.5, pages[t][:, cols], ALU.mult, ALU.add)

        def store_pair(u, q):
            nc.sync.dma_start(out_rows[:, 2 * u : 2 * u + 2, q * QW : (q + 1) * QW], y[q][:, 2 * u : 2 * u + 2, :])

        def round_y(q, on_vector):
            dst = y_bf[q][:].rearrange("p (c i) t -> p c t i", i=4)
            src = y[q][:].rearrange("p t (c i) -> p c t i", i=4)
            if on_vector:
                nc.vector.tensor_copy(dst, src)
            else:
                nc.scalar.copy(dst, src)

        def quantize_y(q):
            cols = slice(q * QW, (q + 1) * QW)
            nc.vector.quantize_mx(
                out=y_codes[:, cols].bitcast(E4M3),
                scales=y_plane[:, cols],
                in_=y_bf[q][:].rearrange("p c t -> p (c t)"),
            )
            nc.sync.dma_start(out_1[0].rearrange("p c t -> p (c t)").bitcast(I32)[:, cols], y_codes[:, cols].bitcast(I32))

        for c in range(CHUNKS):
            weave_h(c)
            second_product(c)
            scatter(1, c, False)
        for c in range(CHUNKS):
            scatter(0, c, True)
        scatter(3, 2, True)
        scatter(3, 1, True)
        for c in range(CHUNKS):
            scatter(2, c, False)
        scatter(3, 0, False)
        for q in range(QUARTERS):
            add_old(0, q)
            add_old(1, q)
            store_pair(0, q)
        for q in range(QUARTERS):
            add_old(2, q)
            add_old(3, q)
            store_pair(1, q)
            if q + 1 < QUARTERS:
                round_y(q, False)
        quantize_y(0)
        round_y(QUARTERS - 1, True)
        quantize_y(1)
        quantize_y(3)
        quantize_y(2)
        for q in range(4):
            queue = nc.sync if q % 2 == 0 else nc.scalar
            queue.dma_start(out_2[0, 4 * q : 4 * q + 4, :].bitcast(I32), y_plane[32 * q : 32 * q + 4, :].bitcast(I32))
